import numpy as np
import ml_dtypes


def mxq(x, axis, fmt="e4m3"):
    dtype, down = {"e4m3": (ml_dtypes.float8_e4m3fn, 7), "e5m2": (ml_dtypes.float8_e5m2, 14)}[fmt]
    v = np.moveaxis(np.asarray(x, np.float32).astype(ml_dtypes.bfloat16).astype(np.float64), axis, -1)
    blocks = v.reshape(v.shape[:-1] + (-1, 32))
    amax = np.abs(blocks).max(-1, keepdims=True)
    byte = np.maximum(np.where(amax > 0, np.frexp(amax)[1] - 1 + 127, 0) - down, 1)
    scale = np.exp2(byte - 127.0)
    codes = (blocks / scale).astype(np.float32).astype(dtype).astype(np.float64)
    return np.moveaxis((codes * scale).reshape(v.shape), -1, axis)


WIDE = False


def mx_kscale(k):
    if not WIDE:
        return np.ones(k)
    levels = np.array([10, -10, 5, -5, 0])
    if k % 512:
        return np.exp2(np.random.permutation(np.resize(levels, k // 32))).repeat(32)
    a = np.empty((k // 512, 16))
    for p in range(k // 512):
        a[p, :8] = np.random.permutation(np.resize(levels, 8))
        for g in range(8):
            far = levels[np.abs(levels - a[p, g]) >= 10]
            a[p, g + 8] = far[np.random.randint(len(far))]
    return np.exp2(a.ravel()).repeat(32)


def f64(x):
    return np.asarray(x).astype(np.float64)


def striped8(idx):
    return np.asarray(idx).reshape(8, -1, 16).transpose(0, 2, 1).reshape(128, -1).astype(np.uint16)


def unstriped8(offs):
    return offs.reshape(8, 16, -1).transpose(0, 2, 1).reshape(8, -1).astype(np.int64)


def pick8(x, idx, run):
    r = np.arange(len(x))
    return x[r[:, None], idx[r % (8 * run) // run]]


E2M1 = np.array([0.0, 0.5, 1.0, 1.5, 2.0, 3.0, 4.0, 6.0, -0.0, -0.5, -1.0, -1.5, -2.0, -3.0, -4.0, -6.0])


def pack_weight(w, fmt):
    k, n = w.shape
    w = f64(np.asarray(w, np.float32).astype(ml_dtypes.bfloat16)).reshape(k // 32, 32, n)
    amax = np.abs(w).max(1)
    if fmt == "e4m3":
        byte = np.frexp(amax)[1] - 1 + 127 - 7
    else:
        mant, ex = np.frexp(amax / 6.0)
        byte = np.where(mant > 0.5, ex, ex - 1) + 127
    byte = np.clip(np.where(amax > 0, byte, 1), 1, 254)
    scaled = (w * np.exp2(127.0 - byte)[:, None, :]).reshape(k, n).astype(np.float32)
    by_word = np.ascontiguousarray(scaled.reshape(k // 512, 128, 4, n).transpose(0, 1, 3, 2))
    if fmt == "e4m3":
        words = by_word.astype(ml_dtypes.float8_e4m3fn).view(np.uint8)
    else:
        c = by_word.astype(ml_dtypes.float4_e2m1fn).view(np.uint8) & 0xF
        words = (c[..., 0::2] | (c[..., 1::2] << 4)).reshape(k // 512, 128, 2 * n)
    return np.ascontiguousarray(words), np.ascontiguousarray(byte.astype(np.uint8).reshape(k // 512, 16, n))


def unpack_weight(words, scales, fmt):
    g, _, n = scales.shape
    words = np.ascontiguousarray(words).reshape(g, 128, n, -1)
    if fmt == "e4m3":
        vals = words.view(ml_dtypes.float8_e4m3fn).astype(np.float64)
    else:
        nib = np.empty((g, 128, n, 4), np.uint8)
        nib[..., 0::2] = words & 0xF
        nib[..., 1::2] = words >> 4
        vals = E2M1[nib]
    vals = vals * np.repeat(np.exp2(scales.astype(np.float64) - 127.0), 8, axis=1)[..., None]
    return vals.transpose(0, 1, 3, 2).reshape(g * 512, n)


def sigmoid(v):
    return 1.0 / (1.0 + np.exp(-v))


K, T, J, N, L = 512, 1024, 256, 512, 512


def setup_inputs():
    n = np.random.standard_normal
    idx = np.stack([np.random.permutation(T)[:J] for _ in range(8)])
    fk = mx_kscale(K)
    fl = mx_kscale(L)
    xvp = pack_weight(n((K, J)) / fk[:, None], "e4m3")
    xgp = pack_weight(n((L, J)) / fl[:, None], "e2m1")
    wgp = pack_weight(n((L, N)) * 1 / np.sqrt(L) * fl[:, None], "e4m3")
    return {
        "xv_words": xvp[0],
        "xv_scales": xvp[1],
        "wv": (n((K, N)) * 1 / np.sqrt(K) * fk[:, None]).astype(np.float32),
        "xg_words": xgp[0],
        "xg_scales": xgp[1],
        "wg_words": wgp[0],
        "wg_scales": wgp[1],
        "old": (1.0 * n((N, T))).astype(np.float32),
        "offs": striped8(idx),
    }


def reference(xv_words, xv_scales, wv, xg_words, xg_scales, wg_words, wg_scales, old, offs):
    idx = unstriped8(offs)
    xvu = unpack_weight(xv_words, xv_scales, "e4m3")
    xgu = unpack_weight(xg_words, xg_scales, "e2m1")
    wgu = unpack_weight(wg_words, wg_scales, "e4m3")
    wvq = mxq(f64(wv), 0, "e4m3")
    v = wvq.T @ xvu
    g = wgu.T @ xgu
    d = sigmoid(g) * (v - pick8(f64(old), idx, 64))
    p = np.zeros((N, T))
    p[np.arange(N)[:, None], idx[np.arange(N) % 512 // 64]] = d
    y = f64(old) + p
    return y

@@ -1,0 +1,150 @@
+from contextlib import ExitStack
+
+import concourse.mybir as mybir
+
+K, T, J, N, L = 512, 1024, 256, 512, 512
+FLOPS = 2 * K * N * J + 2 * L * N * J
+
+F32 = mybir.dt.float32
+BF16 = mybir.dt.bfloat16
+I32 = mybir.dt.int32
+U32 = mybir.dt.uint32
+U16 = mybir.dt.uint16
+U8 = mybir.dt.uint8
+FP8X4 = mybir.dt.float8_e4m3fn_x4
+FP4X4 = mybir.dt.float4_e2m1fn_x4
+ALU = mybir.AluOpType
+ACT = mybir.ActivationFunctionType
+
+P = 128
+R = 4
+M = 128
+
+
+def load_scales(queue, plane, scales):
+    rows = scales[0].bitcast(I32)
+    width = rows.shape[1]
+    words = plane[:].bitcast(I32)
+    for q in range(4):
+        spread = rows[4 * q : 4 * q + 4, :].unsqueeze(0).to_broadcast([8, 4, width])
+        queue.dma_start(words[32 * q : 32 * q + 32, :], spread)
+
+
+def tile_list_head_page_drift_kernel(tc, xv_words, xv_scales, wv, xg_words, xg_scales, wg_words, wg_scales, old, offs, out):
+    nc = tc.nc
+    with ExitStack() as ctx:
+        keep = ctx.enter_context(tc.tile_pool(name="keep", bufs=1))
+        psum = ctx.enter_context(tc.psum_pool(name="psum", bufs=1))
+
+        offsets = keep.tile([P, J // 16], U16, name="offsets")
+        wv_raw = keep.tile([P, 4, N], F32, name="wv_raw")
+        wv_bf = keep.tile([P, R, M, 4], BF16, name="wv_bf", align_bytes=64)
+        wv_codes = keep.tile([P, N], U32, name="wv_codes", align_bytes=64)
+        wv_plane = keep.tile([P, N], U8, name="wv_plane", align_bytes=64)
+        wg_raw = keep.tile([P, N], I32, name="wg_raw")
+        wg_plane_raw = keep.tile([P, N], U8, name="wg_plane_raw")
+        wg_codes = keep.tile([P, N], I32, name="wg_codes", align_bytes=64)
+        wg_plane = keep.tile([P, N], U8, name="wg_plane", align_bytes=64)
+        xv_codes = keep.tile([P, J], I32, name="xv_codes", align_bytes=64)
+        xv_plane = keep.tile([P, J], U8, name="xv_plane", align_bytes=64)
+        xg_codes = keep.tile([P, 2 * J], U8, name="xg_codes", align_bytes=64)
+        xg_plane = keep.tile([P, J], U8, name="xg_plane", align_bytes=64)
+        pages = [keep.tile([P, T], F32, name=f"page{r}") for r in range(R)]
+        drifts = [keep.tile([P, T], F32, name=f"drift{r}") for r in range(R)]
+        results = [keep.tile([P, T], F32, name=f"result{r}") for r in range(R)]
+        gates = [keep.tile([P, 2 * J], F32, name=f"gate{h}") for h in range(2)]
+        neg_gates = [keep.tile([P, 2 * J], F32, name=f"neg_gate{h}") for h in range(2)]
+        values = [keep.tile([P, J], F32, name=f"value{r}") for r in range(R)]
+        gaps = [keep.tile([P, J], F32, name=f"gap{r}") for r in range(R)]
+        warm = keep.tile([P, 8], F32, name="warm")
+        g_banks = [psum.tile([P, 2 * J], F32, name=f"g_bank{h}") for h in range(2)]
+        v_banks = [psum.tile([P, J], F32, name=f"v_bank{r}") for r in range(R)]
+
+        old_rows = old.rearrange("(p r) t -> r p t", r=R)
+        out_rows = out.rearrange("(p r) t -> r p t", r=R)
+
+        nc.sync.dma_start(offsets[:], offs)
+        load_scales(nc.sync, wg_plane_raw, wg_scales)
+        nc.sync.dma_start(xg_codes[:].bitcast(I32), xg_words[0].bitcast(I32))
+        nc.sync.dma_start(wg_raw[:], wg_words[0].rearrange("p n t -> p (n t)").bitcast(I32))
+        nc.sync.dma_start(wv_raw[:], wv.rearrange("(p j) n -> p j n", j=4))
+        load_scales(nc.gpsimd, xg_plane, xg_scales)
+        load_scales(nc.sync, xv_plane, xv_scales)
+        nc.sync.dma_start(xv_codes[:], xv_words[0].rearrange("p n t -> p (n t)").bitcast(I32))
+        for r in range(R):
+            nc.sync.dma_start(pages[r][:], old_rows[r])
+
+        for r in range(R):
+            nc.vector.memset(drifts[r][:], 0.0)
+        nc.scalar.activation(warm[:, 0:1], drifts[0][:, 0:1], ACT.Sigmoid)
+
+        nc.vector.tensor_copy(
+            out=wg_codes[:].rearrange("p (r c i) -> p c r i", r=R, i=4),
+            in_=wg_raw[:].rearrange("p (c i r) -> p c r i", r=R, i=4),
+        )
+        nc.vector.tensor_copy(
+            out=wg_plane[:].rearrange("p (r m) -> p r m", r=R),
+            in_=wg_plane_raw[:].rearrange("p (m r) -> p r m", r=R),
+        )
+        for r in range(R):
+            cols = slice(r * M, (r + 1) * M)
+            nc.tensor.matmul_mx(
+                out=g_banks[r // 2][:, (r % 2) * J : (r % 2 + 1) * J],
+                lhsT=wg_codes[:, cols].bitcast(FP8X4),
+                lhsT_scale=wg_plane[:, cols],
+                rhs=xg_codes[:].bitcast(FP4X4),
+                rhs_scale=xg_plane[:],
+                start=True,
+                stop=True,
+            )
+        for h in range(2):
+            nc.scalar.activation(gates[h][:], g_banks[h][:], ACT.Sigmoid)
+            nc.scalar.activation(neg_gates[h][:], gates[h][:], ACT.Copy, scale=-1.0)
+
+        split = 80
+        src = wv_raw[:].rearrange("p j (m r) -> p m r j", r=R)
+        dst = wv_bf[:].rearrange("p r m j -> p m r j")
+        nc.vector.tensor_copy(out=dst[:, :split], in_=src[:, :split])
+        nc.scalar.copy(out=dst[:, split:], in_=src[:, split:])
+        for lo, hi in ((0, 1), (1, 2), (2, 4)):
+            nc.vector.quantize_mx(
+                out=wv_codes[:, lo * M : hi * M].bitcast(FP8X4),
+                scales=wv_plane[:, lo * M : hi * M],
+                in_=wv_bf[:, lo:hi].rearrange("p r m j -> p (r m j)"),
+            )
+        for r in range(R):
+            cols = slice(r * M, (r + 1) * M)
+            nc.tensor.matmul_mx(
+                out=v_banks[r][:],
+                lhsT=wv_codes[:, cols].bitcast(FP8X4),
+                lhsT_scale=wv_plane[:, cols],
+                rhs=xv_codes[:].bitcast(FP8X4),
+                rhs_scale=xv_plane[:],
+                start=True,
+                stop=True,
+            )
+            nc.scalar.copy(out=values[r][:], in_=v_banks[r][:])
+
+        def gather(r):
+            nc.vector.tensor_tensor(gaps[r][:], pages[r][:].indirect(offsets[:]), values[r][:], ALU.subtract)
+
+        def scatter(r):
+            nc.vector.tensor_tensor(
+                drifts[r][:].indirect(offsets[:]), gaps[r][:], neg_gates[r // 2][:, (r % 2) * J : (r % 2 + 1) * J], ALU.mult
+            )
+
+        def add_and_store(r, pieces):
+            width = T // pieces
+            for c in range(pieces):
+                cols = slice(c * width, (c + 1) * width)
+                nc.vector.tensor_tensor(results[r][:, cols], pages[r][:, cols], drifts[r][:, cols], ALU.add)
+                nc.sync.dma_start(out_rows[r][:, cols], results[r][:, cols])
+
+        gather(0)
+        for r in range(R):
+            if r + 1 < R:
+                gather(r + 1)
+            scatter(r)
+            if r > 0:
+                add_and_store(r - 1, 1)
+        add_and_store(R - 1, 2)

@@ -1,6 +1,7 @@
 from contextlib import ExitStack
 
 import concourse.mybir as mybir
+from concourse.masks import make_identity
 
 K, T, J, N, L = 512, 1024, 256, 512, 512
 FLOPS = 2 * K * N * J + 2 * L * N * J
@@ -19,15 +20,22 @@ ACT = mybir.ActivationFunctionType
 P = 128
 R = 4
 M = 128
+BANK = 512
 
 
-def load_scales(queue, plane, scales):
+def load_scales_repeated(queue, plane, scales, quadrants):
     rows = scales[0].bitcast(I32)
-    width = rows.shape[1]
     words = plane[:].bitcast(I32)
-    for q in range(4):
-        spread = rows[4 * q : 4 * q + 4, :].unsqueeze(0).to_broadcast([8, 4, width])
+    for q in quadrants:
+        spread = rows[4 * q : 4 * q + 4, :].unsqueeze(0).to_broadcast([8, 4, rows.shape[1]])
         queue.dma_start(words[32 * q : 32 * q + 32, :], spread)
+
+
+def load_scales(queue, plane, scales, quadrants):
+    rows = scales[0].bitcast(I32)
+    words = plane[:].bitcast(I32)
+    for q in quadrants:
+        queue.dma_start(words[32 * q : 32 * q + 4, :], rows[4 * q : 4 * q + 4, :])
 
 
 def tile_list_head_page_drift_kernel(tc, xv_words, xv_scales, wv, xg_words, xg_scales, wg_words, wg_scales, old, offs, out):
@@ -41,7 +49,7 @@ def tile_list_head_page_drift_kernel(tc, xv_words, xv_scales, wv, xg_words, xg_s
         wv_bf = keep.tile([P, R, M, 4], BF16, name="wv_bf", align_bytes=64)
         wv_codes = keep.tile([P, N], U32, name="wv_codes", align_bytes=64)
         wv_plane = keep.tile([P, N], U8, name="wv_plane", align_bytes=64)
-        wg_raw = keep.tile([P, N], I32, name="wg_raw")
+        wg_raw = keep.tile([P, N], I32, name="wg_raw", tag="then_identity")
         wg_plane_raw = keep.tile([P, N], U8, name="wg_plane_raw")
         wg_codes = keep.tile([P, N], I32, name="wg_codes", align_bytes=64)
         wg_plane = keep.tile([P, N], U8, name="wg_plane", align_bytes=64)
@@ -50,34 +58,46 @@ def tile_list_head_page_drift_kernel(tc, xv_words, xv_scales, wv, xg_words, xg_s
         xg_codes = keep.tile([P, 2 * J], U8, name="xg_codes", align_bytes=64)
         xg_plane = keep.tile([P, J], U8, name="xg_plane", align_bytes=64)
         pages = [keep.tile([P, T], F32, name=f"page{r}") for r in range(R)]
-        drifts = [keep.tile([P, T], F32, name=f"drift{r}") for r in range(R)]
         results = [keep.tile([P, T], F32, name=f"result{r}") for r in range(R)]
-        gates = [keep.tile([P, 2 * J], F32, name=f"gate{h}") for h in range(2)]
-        neg_gates = [keep.tile([P, 2 * J], F32, name=f"neg_gate{h}") for h in range(2)]
-        values = [keep.tile([P, J], F32, name=f"value{r}") for r in range(R)]
+        gates = keep.tile([P, R, J], F32, name="gates")
+        picked = keep.tile([P, J], F32, name="picked")
+        values = keep.tile([P, R, J], F32, name="values")
+        neg_gates = keep.tile([P, R, J], F32, name="neg_gates")
         gaps = [keep.tile([P, J], F32, name=f"gap{r}") for r in range(R)]
         warm = keep.tile([P, 8], F32, name="warm")
-        g_banks = [psum.tile([P, 2 * J], F32, name=f"g_bank{h}") for h in range(2)]
-        v_banks = [psum.tile([P, J], F32, name=f"v_bank{r}") for r in range(R)]
+        g_banks = [psum.tile([P, 2, J], F32, name=f"g_bank{h}", tag=f"bank{h}") for h in range(2)]
+        v_banks = [psum.tile([P, 2, J], F32, name=f"v_bank{h}", tag=f"bank{2 + h}") for h in range(3)]
+        v_of = [v_banks[0][:, 0, :], v_banks[1][:, 0, :], v_banks[2][:, 0, :], v_banks[2][:, 1, :]]
 
         old_rows = old.rearrange("(p r) t -> r p t", r=R)
         out_rows = out.rearrange("(p r) t -> r p t", r=R)
 
-        nc.sync.dma_start(offsets[:], offs)
-        load_scales(nc.sync, wg_plane_raw, wg_scales)
-        nc.sync.dma_start(xg_codes[:].bitcast(I32), xg_words[0].bitcast(I32))
         nc.sync.dma_start(wg_raw[:], wg_words[0].rearrange("p n t -> p (n t)").bitcast(I32))
+        load_scales_repeated(nc.sync, wg_plane_raw, wg_scales, range(0, 4))
+        load_scales_repeated(nc.sync, xv_plane, xv_scales, range(0, 2))
         nc.sync.dma_start(wv_raw[:], wv.rearrange("(p j) n -> p j n", j=4))
-        load_scales(nc.gpsimd, xg_plane, xg_scales)
-        load_scales(nc.sync, xv_plane, xv_scales)
+        nc.gpsimd.memset(xg_plane[:].bitcast(U32), 0)
+        load_scales(nc.gpsimd, xg_plane, xg_scales, range(1, 4))
+        load_scales_repeated(nc.sync, xv_plane, xv_scales, range(2, 4))
+        load_scales(nc.sync, xg_plane, xg_scales, range(0, 1))
+        nc.sync.dma_start(offsets[:], offs)
+        nc.sync.dma_start(xg_codes[:].bitcast(I32), xg_words[0].bitcast(I32))
         nc.sync.dma_start(xv_codes[:], xv_words[0].rearrange("p n t -> p (n t)").bitcast(I32))
-        for r in range(R):
-            nc.sync.dma_start(pages[r][:], old_rows[r])
+        nc.sync.dma_start(pages[0][:], old_rows[0])
+        nc.sync.dma_start(pages[1][:], old_rows[1])
+        nc.sync.dma_start(pages[2][:], old_rows[2])
+        nc.sync.dma_start(pages[3][:], old_rows[3])
 
-        for r in range(R):
-            nc.vector.memset(drifts[r][:], 0.0)
+        drifts = {0: keep.tile([P, T], F32, name="drift0", tag="then_drift1")}
+        nc.vector.memset(drifts[0][:, : T // 2 - 1], 0.0)
+        nc.vector.memset(drifts[0][:, T // 2 - 1 :], 0.0)
         nc.scalar.activation(warm[:, 0:1], drifts[0][:, 0:1], ACT.Sigmoid)
 
+        split = 80
+        src = wv_raw[:].rearrange("p j (m r) -> p m r j", r=R)
+        dst = wv_bf[:].rearrange("p r m j -> p m r j")
+        nc.vector.tensor_copy(out=dst[:, :split], in_=src[:, :split])
+        nc.scalar.copy(out=dst[:, split:], in_=src[:, split:])
         nc.vector.tensor_copy(
             out=wg_codes[:].rearrange("p (r c i) -> p c r i", r=R, i=4),
             in_=wg_raw[:].rearrange("p (c i r) -> p c r i", r=R, i=4),
@@ -86,10 +106,20 @@ def tile_list_head_page_drift_kernel(tc, xv_words, xv_scales, wv, xg_words, xg_s
             out=wg_plane[:].rearrange("p (r m) -> p r m", r=R),
             in_=wg_plane_raw[:].rearrange("p (m r) -> p r m", r=R),
         )
-        for r in range(R):
+        identity = keep.tile([P, P], F32, name="identity", tag="then_identity")
+        make_identity(nc, identity[:])
+
+        for lo, hi in ((0, 1), (1, 2), (2, 4)):
+            nc.vector.quantize_mx(
+                out=wv_codes[:, lo * M : hi * M].bitcast(FP8X4),
+                scales=wv_plane[:, lo * M : hi * M],
+                in_=wv_bf[:, lo:hi].rearrange("p r m j -> p (r m j)"),
+            )
+
+        def gate_product(r):
             cols = slice(r * M, (r + 1) * M)
             nc.tensor.matmul_mx(
-                out=g_banks[r // 2][:, (r % 2) * J : (r % 2 + 1) * J],
+                out=g_banks[r // 2][:, r % 2, :],
                 lhsT=wg_codes[:, cols].bitcast(FP8X4),
                 lhsT_scale=wg_plane[:, cols],
                 rhs=xg_codes[:].bitcast(FP4X4),
@@ -97,25 +127,11 @@ def tile_list_head_page_drift_kernel(tc, xv_words, xv_scales, wv, xg_words, xg_s
                 start=True,
                 stop=True,
             )
-        for h in range(2):
-            nc.scalar.activation(gates[h][:], g_banks[h][:], ACT.Sigmoid)
-            nc.scalar.activation(neg_gates[h][:], gates[h][:], ACT.Copy, scale=-1.0)
 
-        split = 80
-        src = wv_raw[:].rearrange("p j (m r) -> p m r j", r=R)
-        dst = wv_bf[:].rearrange("p r m j -> p m r j")
-        nc.vector.tensor_copy(out=dst[:, :split], in_=src[:, :split])
-        nc.scalar.copy(out=dst[:, split:], in_=src[:, split:])
-        for lo, hi in ((0, 1), (1, 2), (2, 4)):
-            nc.vector.quantize_mx(
-                out=wv_codes[:, lo * M : hi * M].bitcast(FP8X4),
-                scales=wv_plane[:, lo * M : hi * M],
-                in_=wv_bf[:, lo:hi].rearrange("p r m j -> p (r m j)"),
-            )
-        for r in range(R):
+        def value_product(r):
             cols = slice(r * M, (r + 1) * M)
             nc.tensor.matmul_mx(
-                out=v_banks[r][:],
+                out=v_of[r],
                 lhsT=wv_codes[:, cols].bitcast(FP8X4),
                 lhsT_scale=wv_plane[:, cols],
                 rhs=xv_codes[:].bitcast(FP8X4),
@@ -123,28 +139,73 @@ def tile_list_head_page_drift_kernel(tc, xv_words, xv_scales, wv, xg_words, xg_s
                 start=True,
                 stop=True,
             )
-            nc.scalar.copy(out=values[r][:], in_=v_banks[r][:])
 
-        def gather(r):
-            nc.vector.tensor_tensor(gaps[r][:], pages[r][:].indirect(offsets[:]), values[r][:], ALU.subtract)
+        value_product(0)
+        for h in range(2):
+            gate_product(2 * h)
+            gate_product(2 * h + 1)
+            nc.scalar.activation(gates[:, 2 * h : 2 * h + 2, :], g_banks[h][:], ACT.Sigmoid)
+            value_product(h + 1)
+        value_product(3)
 
-        def scatter(r):
+        def gather_gap(r):
+            nc.vector.tensor_tensor(gaps[r][:], pages[r][:].indirect(offsets[:]), values[:, r, :], ALU.subtract)
+
+        def scatter(r, factor, lo, hi):
             nc.vector.tensor_tensor(
-                drifts[r][:].indirect(offsets[:]), gaps[r][:], neg_gates[r // 2][:, (r % 2) * J : (r % 2 + 1) * J], ALU.mult
+                drifts[r][:].indirect(offsets[:, lo // 16 : hi // 16]), gaps[r][:, lo:hi], factor[:, r, lo:hi], ALU.mult
             )
 
-        def add_and_store(r, pieces):
-            width = T // pieces
-            for c in range(pieces):
-                cols = slice(c * width, (c + 1) * width)
-                nc.vector.tensor_tensor(results[r][:, cols], pages[r][:, cols], drifts[r][:, cols], ALU.add)
-                nc.sync.dma_start(out_rows[r][:, cols], results[r][:, cols])
+        def add_and_store(r, lo, hi):
+            nc.vector.tensor_tensor(results[r][:, lo:hi], pages[r][:, lo:hi], drifts[r][:, lo:hi], ALU.add)
+            nc.sync.dma_start(out_rows[r][:, lo:hi], results[r][:, lo:hi])
 
-        gather(0)
-        for r in range(R):
-            if r + 1 < R:
-                gather(r + 1)
-            scatter(r)
-            if r > 0:
-                add_and_store(r - 1, 1)
-        add_and_store(R - 1, 2)
+        def add_on_tensor_and_store(r, sum_tags, back_tags, whole):
+            blocks = BANK // P
+            halves = range(len(sum_tags))
+            sums = [psum.tile([P, blocks, P], F32, name=f"sums{r}{h}", tag=sum_tags[h]) for h in halves]
+            for k, term in enumerate((pages[r], drifts[r])):
+                for h in halves:
+                    for b in range(blocks):
+                        cols = slice(h * BANK + b * P, h * BANK + (b + 1) * P)
+                        nc.tensor.matmul(
+                            sums[h][:, b, :], term[:, cols], identity[:], is_transpose=True,
+                            start=(k == 0 and b == 0), stop=(k == 1 and b == blocks - 1),
+                        )
+            turned = [keep.tile([P, blocks, P], F32, name=f"turned{r}{h}", tag=f"then_drift{2 + h}" if r == 0 else f"turned{r}{h}") for h in halves]
+            for h in halves:
+                nc.scalar.copy(out=turned[h][:], in_=sums[h][:])
+            for h in halves:
+                back = psum.tile([P, blocks, P], F32, name=f"back{r}{h}", tag=back_tags[h])
+                for b in range(blocks):
+                    nc.tensor.transpose(back[:, b, :], turned[h][:, b, :], identity[:])
+                cols = slice(h * BANK, (h + 1) * BANK)
+                nc.scalar.copy(out=results[r][:, cols], in_=back[:].rearrange("p b c -> p (b c)"))
+                if not whole:
+                    nc.scalar.dma_start(out_rows[r][:, cols], results[r][:, cols])
+            if whole:
+                nc.scalar.dma_start(out_rows[r], results[r][:])
+
+        def clear(r):
+            drifts[r] = keep.tile([P, T], F32, name=f"drift{r}", tag=f"then_drift{r}")
+            nc.gpsimd.memset(drifts[r][:], 0.0)
+
+        nc.vector.tensor_copy(picked[:], pages[0][:].indirect(offsets[:]))
+        nc.vector.tensor_tensor(gaps[0][:], v_of[0], picked[:], ALU.subtract)
+        scatter(0, gates, 0, J)
+        nc.scalar.copy(out=values[:, 1, :], in_=v_of[1])
+        nc.scalar.copy(out=values[:, 2:4, :], in_=v_banks[2][:])
+        nc.scalar.activation(neg_gates[:, 1:4, :], gates[:, 1:4, :], ACT.Copy, scale=-1.0)
+        back_tags = ("bank5", "bank6")
+        add_on_tensor_and_store(0, ("bank2", "bank0"), back_tags, True)
+        for r in range(1, R):
+            clear(r)
+            gather_gap(r)
+        scatter(1, neg_gates, 0, J)
+        add_on_tensor_and_store(1, ("bank1", "bank3"), back_tags, False)
+        scatter(2, neg_gates, 0, J)
+        add_on_tensor_and_store(2, ("bank4",), back_tags, False)
+        add_and_store(2, BANK, T)
+        scatter(3, neg_gates, 0, J)
+        add_and_store(3, 0, T // 2)
+        add_and_store(3, T // 2, T)

@@ -49,8 +49,8 @@ def tile_list_head_page_drift_kernel(tc, xv_words, xv_scales, wv, xg_words, xg_s
         wv_bf = keep.tile([P, R, M, 4], BF16, name="wv_bf", align_bytes=64)
         wv_codes = keep.tile([P, N], U32, name="wv_codes", align_bytes=64)
         wv_plane = keep.tile([P, N], U8, name="wv_plane", align_bytes=64)
-        wg_raw = keep.tile([P, N], I32, name="wg_raw", tag="then_identity")
-        wg_plane_raw = keep.tile([P, N], U8, name="wg_plane_raw")
+        wg_raw = keep.tile([P, N], I32, name="wg_raw", tag="then_drift2")
+        wg_plane_raw = keep.tile([P, N], U8, name="wg_plane_raw", tag="then_drift3")
         wg_codes = keep.tile([P, N], I32, name="wg_codes", align_bytes=64)
         wg_plane = keep.tile([P, N], U8, name="wg_plane", align_bytes=64)
         xv_codes = keep.tile([P, J], I32, name="xv_codes", align_bytes=64)
@@ -62,7 +62,6 @@ def tile_list_head_page_drift_kernel(tc, xv_words, xv_scales, wv, xg_words, xg_s
         gates = keep.tile([P, R, J], F32, name="gates")
         picked = keep.tile([P, J], F32, name="picked")
         values = keep.tile([P, R, J], F32, name="values")
-        neg_gates = keep.tile([P, R, J], F32, name="neg_gates")
         gaps = [keep.tile([P, J], F32, name=f"gap{r}") for r in range(R)]
         warm = keep.tile([P, 8], F32, name="warm")
         g_banks = [psum.tile([P, 2, J], F32, name=f"g_bank{h}", tag=f"bank{h}") for h in range(2)]
@@ -72,11 +71,11 @@ def tile_list_head_page_drift_kernel(tc, xv_words, xv_scales, wv, xg_words, xg_s
         old_rows = old.rearrange("(p r) t -> r p t", r=R)
         out_rows = out.rearrange("(p r) t -> r p t", r=R)
 
+        nc.vector.memset(xg_plane[:].bitcast(U32), 0)
         nc.sync.dma_start(wg_raw[:], wg_words[0].rearrange("p n t -> p (n t)").bitcast(I32))
         load_scales_repeated(nc.sync, wg_plane_raw, wg_scales, range(0, 4))
         load_scales_repeated(nc.sync, xv_plane, xv_scales, range(0, 2))
         nc.sync.dma_start(wv_raw[:], wv.rearrange("(p j) n -> p j n", j=4))
-        nc.gpsimd.memset(xg_plane[:].bitcast(U32), 0)
         load_scales(nc.gpsimd, xg_plane, xg_scales, range(1, 4))
         load_scales_repeated(nc.sync, xv_plane, xv_scales, range(2, 4))
         load_scales(nc.sync, xg_plane, xg_scales, range(0, 1))
@@ -88,10 +87,13 @@ def tile_list_head_page_drift_kernel(tc, xv_words, xv_scales, wv, xg_words, xg_s
         nc.sync.dma_start(pages[2][:], old_rows[2])
         nc.sync.dma_start(pages[3][:], old_rows[3])
 
-        drifts = {0: keep.tile([P, T], F32, name="drift0", tag="then_drift1")}
-        nc.vector.memset(drifts[0][:, : T // 2 - 1], 0.0)
-        nc.vector.memset(drifts[0][:, T // 2 - 1 :], 0.0)
-        nc.scalar.activation(warm[:, 0:1], drifts[0][:, 0:1], ACT.Sigmoid)
+        identity = keep.tile([P, P], F32, name="identity")
+        make_identity(nc, identity[:])
+        drifts = [keep.tile([P, T], F32, name=f"drift{r}", tag="then_neg1" if r == 0 else "drift1") for r in range(2)]
+        for r in range(2):
+            nc.vector.memset(drifts[r][:, : T // 2 - 1], 0.0)
+            nc.vector.memset(drifts[r][:, T // 2 - 1 :], 0.0)
+        nc.scalar.activation(warm[:, 0:1], identity[:, 0:1], ACT.Sigmoid)
 
         split = 80
         src = wv_raw[:].rearrange("p j (m r) -> p m r j", r=R)
@@ -106,8 +108,9 @@ def tile_list_head_page_drift_kernel(tc, xv_words, xv_scales, wv, xg_words, xg_s
             out=wg_plane[:].rearrange("p (r m) -> p r m", r=R),
             in_=wg_plane_raw[:].rearrange("p (m r) -> p r m", r=R),
         )
-        identity = keep.tile([P, P], F32, name="identity", tag="then_identity")
-        make_identity(nc, identity[:])
+        for r in range(2, R):
+            drifts.append(keep.tile([P, T], F32, name=f"drift{r}", tag=f"then_drift{r}"))
+            nc.vector.memset(drifts[r][:], 0.0)
 
         for lo, hi in ((0, 1), (1, 2), (2, 4)):
             nc.vector.quantize_mx(
@@ -151,10 +154,8 @@ def tile_list_head_page_drift_kernel(tc, xv_words, xv_scales, wv, xg_words, xg_s
         def gather_gap(r):
             nc.vector.tensor_tensor(gaps[r][:], pages[r][:].indirect(offsets[:]), values[:, r, :], ALU.subtract)
 
-        def scatter(r, factor, lo, hi):
-            nc.vector.tensor_tensor(
-                drifts[r][:].indirect(offsets[:, lo // 16 : hi // 16]), gaps[r][:, lo:hi], factor[:, r, lo:hi], ALU.mult
-            )
+        def scatter(r, factor):
+            nc.vector.tensor_tensor(drifts[r][:].indirect(offsets[:]), gaps[r][:], factor, ALU.mult)
 
         def add_and_store(r, lo, hi):
             nc.vector.tensor_tensor(results[r][:, lo:hi], pages[r][:, lo:hi], drifts[r][:, lo:hi], ALU.add)
@@ -172,7 +173,7 @@ def tile_list_head_page_drift_kernel(tc, xv_words, xv_scales, wv, xg_words, xg_s
                             sums[h][:, b, :], term[:, cols], identity[:], is_transpose=True,
                             start=(k == 0 and b == 0), stop=(k == 1 and b == blocks - 1),
                         )
-            turned = [keep.tile([P, blocks, P], F32, name=f"turned{r}{h}", tag=f"then_drift{2 + h}" if r == 0 else f"turned{r}{h}") for h in halves]
+            turned = [keep.tile([P, blocks, P], F32, name=f"turned{r}{h}", tag=f"then_neg{2 + h}" if r == 0 else f"turned{r}{h}") for h in halves]
             for h in halves:
                 nc.scalar.copy(out=turned[h][:], in_=sums[h][:])
             for h in halves:
@@ -186,26 +187,23 @@ def tile_list_head_page_drift_kernel(tc, xv_words, xv_scales, wv, xg_words, xg_s
             if whole:
                 nc.scalar.dma_start(out_rows[r], results[r][:])
 
-        def clear(r):
-            drifts[r] = keep.tile([P, T], F32, name=f"drift{r}", tag=f"then_drift{r}")
-            nc.gpsimd.memset(drifts[r][:], 0.0)
-
         nc.vector.tensor_copy(picked[:], pages[0][:].indirect(offsets[:]))
         nc.vector.tensor_tensor(gaps[0][:], v_of[0], picked[:], ALU.subtract)
-        scatter(0, gates, 0, J)
+        scatter(0, gates[:, 0, :])
         nc.scalar.copy(out=values[:, 1, :], in_=v_of[1])
         nc.scalar.copy(out=values[:, 2:4, :], in_=v_banks[2][:])
-        nc.scalar.activation(neg_gates[:, 1:4, :], gates[:, 1:4, :], ACT.Copy, scale=-1.0)
         back_tags = ("bank5", "bank6")
         add_on_tensor_and_store(0, ("bank2", "bank0"), back_tags, True)
+        neg_gates = {}
         for r in range(1, R):
-            clear(r)
+            neg_gates[r] = keep.tile([P, J], F32, name=f"neg_gate{r}", tag=f"then_neg{r}")
+            nc.scalar.activation(neg_gates[r][:], gates[:, r, :], ACT.Copy, scale=-1.0)
             gather_gap(r)
-        scatter(1, neg_gates, 0, J)
+        scatter(1, neg_gates[1][:])
         add_on_tensor_and_store(1, ("bank1", "bank3"), back_tags, False)
-        scatter(2, neg_gates, 0, J)
+        scatter(2, neg_gates[2][:])
         add_on_tensor_and_store(2, ("bank4",), back_tags, False)
         add_and_store(2, BANK, T)
-        scatter(3, neg_gates, 0, J)
+        scatter(3, neg_gates[3][:])
         add_and_store(3, 0, T // 2)
         add_and_store(3, T // 2, T)

@@ -71,16 +71,17 @@ def tile_list_head_page_drift_kernel(tc, xv_words, xv_scales, wv, xg_words, xg_s
         old_rows = old.rearrange("(p r) t -> r p t", r=R)
         out_rows = out.rearrange("(p r) t -> r p t", r=R)
 
-        nc.vector.memset(xg_plane[:].bitcast(U32), 0)
+        nc.vector.memset(xv_plane[:].bitcast(U32), 0)
+        nc.vector.memset(xg_plane[64:128, :].bitcast(U32), 0)
         nc.sync.dma_start(wg_raw[:], wg_words[0].rearrange("p n t -> p (n t)").bitcast(I32))
         load_scales_repeated(nc.sync, wg_plane_raw, wg_scales, range(0, 4))
-        load_scales_repeated(nc.sync, xv_plane, xv_scales, range(0, 2))
+        load_scales_repeated(nc.sync, xg_plane, xg_scales, range(0, 2))
         nc.sync.dma_start(wv_raw[:], wv.rearrange("(p j) n -> p j n", j=4))
-        load_scales(nc.gpsimd, xg_plane, xg_scales, range(1, 4))
-        load_scales_repeated(nc.sync, xv_plane, xv_scales, range(2, 4))
-        load_scales(nc.sync, xg_plane, xg_scales, range(0, 1))
-        nc.sync.dma_start(offsets[:], offs)
+        load_scales(nc.gpsimd, xv_plane, xv_scales, range(1, 4))
+        load_scales(nc.sync, xg_plane, xg_scales, range(2, 4))
         nc.sync.dma_start(xg_codes[:].bitcast(I32), xg_words[0].bitcast(I32))
+        load_scales(nc.sync, xv_plane, xv_scales, range(0, 1))
+        nc.sync.dma_start(offsets[:], offs)
         nc.sync.dma_start(xv_codes[:], xv_words[0].rearrange("p n t -> p (n t)").bitcast(I32))
         nc.sync.dma_start(pages[0][:], old_rows[0])
         nc.sync.dma_start(pages[1][:], old_rows[1])
@@ -95,7 +96,7 @@ def tile_list_head_page_drift_kernel(tc, xv_words, xv_scales, wv, xg_words, xg_s
             nc.vector.memset(drifts[r][:, T // 2 - 1 :], 0.0)
         nc.scalar.activation(warm[:, 0:1], identity[:, 0:1], ACT.Sigmoid)
 
-        split = 80
+        split = 68
         src = wv_raw[:].rearrange("p j (m r) -> p m r j", r=R)
         dst = wv_bf[:].rearrange("p r m j -> p m r j")
         nc.vector.tensor_copy(out=dst[:, :split], in_=src[:, :split])
@@ -143,19 +144,20 @@ def tile_list_head_page_drift_kernel(tc, xv_words, xv_scales, wv, xg_words, xg_s
                 stop=True,
             )
 
-        value_product(0)
         for h in range(2):
             gate_product(2 * h)
             gate_product(2 * h + 1)
             nc.scalar.activation(gates[:, 2 * h : 2 * h + 2, :], g_banks[h][:], ACT.Sigmoid)
-            value_product(h + 1)
-        value_product(3)
+        for r in range(R):
+            value_product(r)
 
         def gather_gap(r):
             nc.vector.tensor_tensor(gaps[r][:], pages[r][:].indirect(offsets[:]), values[:, r, :], ALU.subtract)
 
-        def scatter(r, factor):
-            nc.vector.tensor_tensor(drifts[r][:].indirect(offsets[:]), gaps[r][:], factor, ALU.mult)
+        def scatter(r, factor, lo, hi):
+            nc.vector.tensor_tensor(
+                drifts[r][:].indirect(offsets[:, lo // 16 : hi // 16]), gaps[r][:, lo:hi], factor[:, lo:hi], ALU.mult
+            )
 
         def add_and_store(r, lo, hi):
             nc.vector.tensor_tensor(results[r][:, lo:hi], pages[r][:, lo:hi], drifts[r][:, lo:hi], ALU.add)
@@ -173,7 +175,7 @@ def tile_list_head_page_drift_kernel(tc, xv_words, xv_scales, wv, xg_words, xg_s
                             sums[h][:, b, :], term[:, cols], identity[:], is_transpose=True,
                             start=(k == 0 and b == 0), stop=(k == 1 and b == blocks - 1),
                         )
-            turned = [keep.tile([P, blocks, P], F32, name=f"turned{r}{h}", tag=f"then_neg{2 + h}" if r == 0 else f"turned{r}{h}") for h in halves]
+            turned = [keep.tile([P, blocks, P], F32, name=f"turned{r}{h}", tag="then_neg2" if (r, h) == (0, 0) else f"turned{r}{h}") for h in halves]
             for h in halves:
                 nc.scalar.copy(out=turned[h][:], in_=sums[h][:])
             for h in halves:
@@ -189,21 +191,22 @@ def tile_list_head_page_drift_kernel(tc, xv_words, xv_scales, wv, xg_words, xg_s
 
         nc.vector.tensor_copy(picked[:], pages[0][:].indirect(offsets[:]))
         nc.vector.tensor_tensor(gaps[0][:], v_of[0], picked[:], ALU.subtract)
-        scatter(0, gates[:, 0, :])
+        scatter(0, gates[:, 0, :], 0, J)
         nc.scalar.copy(out=values[:, 1, :], in_=v_of[1])
         nc.scalar.copy(out=values[:, 2:4, :], in_=v_banks[2][:])
         back_tags = ("bank5", "bank6")
         add_on_tensor_and_store(0, ("bank2", "bank0"), back_tags, True)
-        neg_gates = {}
+        neg_gate1 = keep.tile([P, J], F32, name="neg_gate1", tag="then_neg1")
+        nc.scalar.activation(neg_gate1[:], gates[:, 1, :], ACT.Copy, scale=-1.0)
+        neg_gates23 = keep.tile([P, 2, J], F32, name="neg_gates23", tag="then_neg2")
+        nc.scalar.activation(neg_gates23[:], gates[:, 2:4, :], ACT.Copy, scale=-1.0)
         for r in range(1, R):
-            neg_gates[r] = keep.tile([P, J], F32, name=f"neg_gate{r}", tag=f"then_neg{r}")
-            nc.scalar.activation(neg_gates[r][:], gates[:, r, :], ACT.Copy, scale=-1.0)
             gather_gap(r)
-        scatter(1, neg_gates[1][:])
+        scatter(1, neg_gate1, 0, J)
         add_on_tensor_and_store(1, ("bank1", "bank3"), back_tags, False)
-        scatter(2, neg_gates[2][:])
-        add_on_tensor_and_store(2, ("bank4",), back_tags, False)
-        add_and_store(2, BANK, T)
-        scatter(3, neg_gates[3][:])
-        add_and_store(3, 0, T // 2)
-        add_and_store(3, T // 2, T)
+        scatter(2, neg_gates23[:, 0, :], 0, J)
+        scatter(3, neg_gates23[:, 1, :], 0, J // 2)
+        add_and_store(2, 0, T)
+        scatter(3, neg_gates23[:, 1, :], J // 2, J)
+        add_and_store(3, 0, 640)
+        add_and_store(3, 640, T)

@@ -18,24 +18,19 @@ ALU = mybir.AluOpType
 ACT = mybir.ActivationFunctionType
 
 P = 128
-R = 4
-M = 128
+PACK = 4
+SLICES = N // P
 BANK = 512
+LINE = 4
+VECTOR_SHARE = 68
+LAST_CUT = 640
 
 
-def load_scales_repeated(queue, plane, scales, quadrants):
+def load_plane(nc, plane, scales):
     rows = scales[0].bitcast(I32)
     words = plane[:].bitcast(I32)
-    for q in quadrants:
-        spread = rows[4 * q : 4 * q + 4, :].unsqueeze(0).to_broadcast([8, 4, rows.shape[1]])
-        queue.dma_start(words[32 * q : 32 * q + 32, :], spread)
-
-
-def load_scales(queue, plane, scales, quadrants):
-    rows = scales[0].bitcast(I32)
-    words = plane[:].bitcast(I32)
-    for q in quadrants:
-        queue.dma_start(words[32 * q : 32 * q + 4, :], rows[4 * q : 4 * q + 4, :])
+    for q in range(4):
+        nc.sync.dma_start(words[32 * q : 32 * q + 4, :], rows[4 * q : 4 * q + 4, :])
 
 
 def tile_list_head_page_drift_kernel(tc, xv_words, xv_scales, wv, xg_words, xg_scales, wg_words, wg_scales, old, offs, out):
@@ -45,137 +40,124 @@ def tile_list_head_page_drift_kernel(tc, xv_words, xv_scales, wv, xg_words, xg_s
         psum = ctx.enter_context(tc.psum_pool(name="psum", bufs=1))
 
         offsets = keep.tile([P, J // 16], U16, name="offsets")
-        wv_raw = keep.tile([P, 4, N], F32, name="wv_raw")
-        wv_bf = keep.tile([P, R, M, 4], BF16, name="wv_bf", align_bytes=64)
+        wv_raw = keep.tile([P, PACK, N], F32, name="wv_raw")
+        wv_bf = keep.tile([P, SLICES, P, PACK], BF16, name="wv_bf", align_bytes=64)
         wv_codes = keep.tile([P, N], U32, name="wv_codes", align_bytes=64)
         wv_plane = keep.tile([P, N], U8, name="wv_plane", align_bytes=64)
-        wg_raw = keep.tile([P, N], I32, name="wg_raw", tag="then_drift2")
-        wg_plane_raw = keep.tile([P, N], U8, name="wg_plane_raw", tag="then_drift3")
+        wg_codes_raw = keep.tile([P, N], I32, name="wg_codes_raw")
+        wg_plane_raw = keep.tile([P, N], U8, name="wg_plane_raw")
         wg_codes = keep.tile([P, N], I32, name="wg_codes", align_bytes=64)
         wg_plane = keep.tile([P, N], U8, name="wg_plane", align_bytes=64)
         xv_codes = keep.tile([P, J], I32, name="xv_codes", align_bytes=64)
         xv_plane = keep.tile([P, J], U8, name="xv_plane", align_bytes=64)
         xg_codes = keep.tile([P, 2 * J], U8, name="xg_codes", align_bytes=64)
         xg_plane = keep.tile([P, J], U8, name="xg_plane", align_bytes=64)
-        pages = [keep.tile([P, T], F32, name=f"page{r}") for r in range(R)]
-        results = [keep.tile([P, T], F32, name=f"result{r}") for r in range(R)]
-        gates = keep.tile([P, R, J], F32, name="gates")
-        picked = keep.tile([P, J], F32, name="picked")
-        values = keep.tile([P, R, J], F32, name="values")
-        gaps = [keep.tile([P, J], F32, name=f"gap{r}") for r in range(R)]
-        warm = keep.tile([P, 8], F32, name="warm")
+        pages = [keep.tile([P, T], F32, name=f"page{r}") for r in range(SLICES)]
+        results = [keep.tile([P, T], F32, name=f"result{r}") for r in range(SLICES)]
+        gates = keep.tile([P, SLICES, J], F32, name="gates")
+        picked0 = keep.tile([P, J], F32, name="picked0")
+        neg_gates = keep.tile([P, SLICES - 1, J], F32, name="neg_gates")
+        value1 = keep.tile([P, J], F32, name="value1", tag="then_drift2")
+        values23 = keep.tile([P, 2, J], F32, name="values23")
+        values = {1: value1[:], 2: values23[:, 0, :], 3: values23[:, 1, :]}
+        gaps = [keep.tile([P, J], F32, name=f"gap{r}", tag="then_drift3" if r == 1 else f"gap{r}") for r in range(SLICES)]
         g_banks = [psum.tile([P, 2, J], F32, name=f"g_bank{h}", tag=f"bank{h}") for h in range(2)]
         v_banks = [psum.tile([P, 2, J], F32, name=f"v_bank{h}", tag=f"bank{2 + h}") for h in range(3)]
-        v_of = [v_banks[0][:, 0, :], v_banks[1][:, 0, :], v_banks[2][:, 0, :], v_banks[2][:, 1, :]]
+        v_psum = [v_banks[0][:, 0, :], v_banks[1][:, 0, :], v_banks[2][:, 0, :], v_banks[2][:, 1, :]]
 
-        old_rows = old.rearrange("(p r) t -> r p t", r=R)
-        out_rows = out.rearrange("(p r) t -> r p t", r=R)
+        old_slices = old.rearrange("(p r) t -> r p t", r=SLICES)
+        out_slices = out.rearrange("(p r) t -> r p t", r=SLICES)
 
-        nc.vector.memset(xv_plane[:].bitcast(U32), 0)
-        nc.vector.memset(xg_plane[64:128, :].bitcast(U32), 0)
-        nc.sync.dma_start(wg_raw[:], wg_words[0].rearrange("p n t -> p (n t)").bitcast(I32))
-        load_scales_repeated(nc.sync, wg_plane_raw, wg_scales, range(0, 4))
-        load_scales_repeated(nc.sync, xg_plane, xg_scales, range(0, 2))
-        nc.sync.dma_start(wv_raw[:], wv.rearrange("(p j) n -> p j n", j=4))
-        load_scales(nc.gpsimd, xv_plane, xv_scales, range(1, 4))
-        load_scales(nc.sync, xg_plane, xg_scales, range(2, 4))
-        nc.sync.dma_start(xg_codes[:].bitcast(I32), xg_words[0].bitcast(I32))
-        load_scales(nc.sync, xv_plane, xv_scales, range(0, 1))
+        for plane in (wg_plane_raw, xv_plane, xg_plane):
+            nc.vector.memset(plane[:].bitcast(U32), 0)
+
+        nc.sync.dma_start(wg_codes_raw[:], wg_words[0].rearrange("p n t -> p (n t)").bitcast(I32))
         nc.sync.dma_start(offsets[:], offs)
+        nc.sync.dma_start(xg_codes[:].bitcast(I32), xg_words[0].bitcast(I32))
+        load_plane(nc, wg_plane_raw, wg_scales)
+        nc.sync.dma_start(wv_raw[:], wv.rearrange("(p j) n -> p j n", j=PACK))
+        load_plane(nc, xg_plane, xg_scales)
         nc.sync.dma_start(xv_codes[:], xv_words[0].rearrange("p n t -> p (n t)").bitcast(I32))
-        nc.sync.dma_start(pages[0][:], old_rows[0])
-        nc.sync.dma_start(pages[1][:], old_rows[1])
-        nc.sync.dma_start(pages[2][:], old_rows[2])
-        nc.sync.dma_start(pages[3][:], old_rows[3])
+        nc.sync.dma_start(pages[0][:], old_slices[0])
+        load_plane(nc, xv_plane, xv_scales)
+        gather_order = (2, 3, 1)
+        for r in gather_order:
+            nc.sync.dma_start(pages[r][:], old_slices[r])
 
         identity = keep.tile([P, P], F32, name="identity")
         make_identity(nc, identity[:])
-        drifts = [keep.tile([P, T], F32, name=f"drift{r}", tag="then_neg1" if r == 0 else "drift1") for r in range(2)]
+        drifts = [keep.tile([P, T], F32, name=f"drift{r}") for r in range(2)]
         for r in range(2):
-            nc.vector.memset(drifts[r][:, : T // 2 - 1], 0.0)
-            nc.vector.memset(drifts[r][:, T // 2 - 1 :], 0.0)
-        nc.scalar.activation(warm[:, 0:1], identity[:, 0:1], ACT.Sigmoid)
-
-        split = 68
-        src = wv_raw[:].rearrange("p j (m r) -> p m r j", r=R)
-        dst = wv_bf[:].rearrange("p r m j -> p m r j")
-        nc.vector.tensor_copy(out=dst[:, :split], in_=src[:, :split])
-        nc.scalar.copy(out=dst[:, split:], in_=src[:, split:])
-        nc.vector.tensor_copy(
-            out=wg_codes[:].rearrange("p (r c i) -> p c r i", r=R, i=4),
-            in_=wg_raw[:].rearrange("p (c i r) -> p c r i", r=R, i=4),
-        )
-        nc.vector.tensor_copy(
-            out=wg_plane[:].rearrange("p (r m) -> p r m", r=R),
-            in_=wg_plane_raw[:].rearrange("p (m r) -> p r m", r=R),
-        )
-        for r in range(2, R):
-            drifts.append(keep.tile([P, T], F32, name=f"drift{r}", tag=f"then_drift{r}"))
             nc.vector.memset(drifts[r][:], 0.0)
+
+        src = wv_raw[:].rearrange("p j (m r) -> p m r j", r=SLICES)
+        dst = wv_bf[:].rearrange("p r m j -> p m r j")
+        nc.vector.tensor_copy(out=dst[:, :VECTOR_SHARE], in_=src[:, :VECTOR_SHARE])
+        nc.scalar.copy(out=dst[:, VECTOR_SHARE:], in_=src[:, VECTOR_SHARE:])
+
+        nc.vector.tensor_copy(
+            out=wg_codes[:].rearrange("p (r c i) -> p c r i", r=SLICES, i=LINE),
+            in_=wg_codes_raw[:].rearrange("p (c i r) -> p c r i", r=SLICES, i=LINE),
+        )
+        nc.vector.tensor_copy(
+            out=wg_plane[:].rearrange("p (r m) -> p r m", r=SLICES),
+            in_=wg_plane_raw[:].rearrange("p (m r) -> p r m", r=SLICES),
+        )
 
         for lo, hi in ((0, 1), (1, 2), (2, 4)):
             nc.vector.quantize_mx(
-                out=wv_codes[:, lo * M : hi * M].bitcast(FP8X4),
-                scales=wv_plane[:, lo * M : hi * M],
+                out=wv_codes[:, lo * P : hi * P].bitcast(FP8X4),
+                scales=wv_plane[:, lo * P : hi * P],
                 in_=wv_bf[:, lo:hi].rearrange("p r m j -> p (r m j)"),
             )
 
-        def gate_product(r):
-            cols = slice(r * M, (r + 1) * M)
+        def product(acc, r, w_codes, w_plane, x_codes, x_plane):
+            cols = slice(r * P, (r + 1) * P)
             nc.tensor.matmul_mx(
-                out=g_banks[r // 2][:, r % 2, :],
-                lhsT=wg_codes[:, cols].bitcast(FP8X4),
-                lhsT_scale=wg_plane[:, cols],
-                rhs=xg_codes[:].bitcast(FP4X4),
-                rhs_scale=xg_plane[:],
-                start=True,
-                stop=True,
-            )
-
-        def value_product(r):
-            cols = slice(r * M, (r + 1) * M)
-            nc.tensor.matmul_mx(
-                out=v_of[r],
-                lhsT=wv_codes[:, cols].bitcast(FP8X4),
-                lhsT_scale=wv_plane[:, cols],
-                rhs=xv_codes[:].bitcast(FP8X4),
-                rhs_scale=xv_plane[:],
+                out=acc,
+                lhsT=w_codes[:, cols].bitcast(FP8X4),
+                lhsT_scale=w_plane[:, cols],
+                rhs=x_codes,
+                rhs_scale=x_plane[:],
                 start=True,
                 stop=True,
             )
 
         for h in range(2):
-            gate_product(2 * h)
-            gate_product(2 * h + 1)
+            for e in range(2):
+                product(g_banks[h][:, e, :], 2 * h + e, wg_codes, wg_plane, xg_codes[:].bitcast(FP4X4), xg_plane)
             nc.scalar.activation(gates[:, 2 * h : 2 * h + 2, :], g_banks[h][:], ACT.Sigmoid)
-        for r in range(R):
-            value_product(r)
+        for r in range(SLICES):
+            product(v_psum[r], r, wv_codes, wv_plane, xv_codes[:].bitcast(FP8X4), xv_plane)
 
-        def gather_gap(r):
-            nc.vector.tensor_tensor(gaps[r][:], pages[r][:].indirect(offsets[:]), values[:, r, :], ALU.subtract)
+        def scatter(r, factor):
+            nc.vector.tensor_tensor(drifts[r][:].indirect(offsets[:]), gaps[r][:], factor, ALU.mult)
 
-        def scatter(r, factor, lo, hi):
-            nc.vector.tensor_tensor(
-                drifts[r][:].indirect(offsets[:, lo // 16 : hi // 16]), gaps[r][:, lo:hi], factor[:, lo:hi], ALU.mult
-            )
+        def clear_late(r):
+            drifts.append(keep.tile([P, T], F32, name=f"drift{r}", tag=f"then_drift{r}"))
+            nc.gpsimd.memset(drifts[r][:], 0.0)
 
-        def add_and_store(r, lo, hi):
+        def add_on_vector(r, lo, hi):
             nc.vector.tensor_tensor(results[r][:, lo:hi], pages[r][:, lo:hi], drifts[r][:, lo:hi], ALU.add)
-            nc.sync.dma_start(out_rows[r][:, lo:hi], results[r][:, lo:hi])
+            nc.sync.dma_start(out_slices[r][:, lo:hi], results[r][:, lo:hi])
 
-        def add_on_tensor_and_store(r, sum_tags, back_tags, whole):
+        def add_on_tensor(r, sum_tags, back_tags):
             blocks = BANK // P
-            halves = range(len(sum_tags))
+            halves = range(T // BANK)
             sums = [psum.tile([P, blocks, P], F32, name=f"sums{r}{h}", tag=sum_tags[h]) for h in halves]
             for k, term in enumerate((pages[r], drifts[r])):
                 for h in halves:
                     for b in range(blocks):
-                        cols = slice(h * BANK + b * P, h * BANK + (b + 1) * P)
+                        first = h * BANK + b * P
                         nc.tensor.matmul(
-                            sums[h][:, b, :], term[:, cols], identity[:], is_transpose=True,
-                            start=(k == 0 and b == 0), stop=(k == 1 and b == blocks - 1),
+                            sums[h][:, b, :],
+                            term[:, first : first + P],
+                            identity[:],
+                            is_transpose=True,
+                            start=(k == 0 and b == 0),
+                            stop=(k == 1 and b == blocks - 1),
                         )
-            turned = [keep.tile([P, blocks, P], F32, name=f"turned{r}{h}", tag="then_neg2" if (r, h) == (0, 0) else f"turned{r}{h}") for h in halves]
+            turned = [keep.tile([P, blocks, P], F32, name=f"turned{r}{h}") for h in halves]
             for h in halves:
                 nc.scalar.copy(out=turned[h][:], in_=sums[h][:])
             for h in halves:
@@ -184,29 +166,25 @@ def tile_list_head_page_drift_kernel(tc, xv_words, xv_scales, wv, xg_words, xg_s
                     nc.tensor.transpose(back[:, b, :], turned[h][:, b, :], identity[:])
                 cols = slice(h * BANK, (h + 1) * BANK)
                 nc.scalar.copy(out=results[r][:, cols], in_=back[:].rearrange("p b c -> p (b c)"))
-                if not whole:
-                    nc.scalar.dma_start(out_rows[r][:, cols], results[r][:, cols])
-            if whole:
-                nc.scalar.dma_start(out_rows[r], results[r][:])
+                nc.scalar.dma_start(out_slices[r][:, cols], results[r][:, cols])
 
-        nc.vector.tensor_copy(picked[:], pages[0][:].indirect(offsets[:]))
-        nc.vector.tensor_tensor(gaps[0][:], v_of[0], picked[:], ALU.subtract)
-        scatter(0, gates[:, 0, :], 0, J)
-        nc.scalar.copy(out=values[:, 1, :], in_=v_of[1])
-        nc.scalar.copy(out=values[:, 2:4, :], in_=v_banks[2][:])
-        back_tags = ("bank5", "bank6")
-        add_on_tensor_and_store(0, ("bank2", "bank0"), back_tags, True)
-        neg_gate1 = keep.tile([P, J], F32, name="neg_gate1", tag="then_neg1")
-        nc.scalar.activation(neg_gate1[:], gates[:, 1, :], ACT.Copy, scale=-1.0)
-        neg_gates23 = keep.tile([P, 2, J], F32, name="neg_gates23", tag="then_neg2")
-        nc.scalar.activation(neg_gates23[:], gates[:, 2:4, :], ACT.Copy, scale=-1.0)
-        for r in range(1, R):
-            gather_gap(r)
-        scatter(1, neg_gate1, 0, J)
-        add_on_tensor_and_store(1, ("bank1", "bank3"), back_tags, False)
-        scatter(2, neg_gates23[:, 0, :], 0, J)
-        scatter(3, neg_gates23[:, 1, :], 0, J // 2)
-        add_and_store(2, 0, T)
-        scatter(3, neg_gates23[:, 1, :], J // 2, J)
-        add_and_store(3, 0, 640)
-        add_and_store(3, 640, T)
+        nc.vector.tensor_copy(picked0[:], pages[0][:].indirect(offsets[:]))
+        nc.vector.tensor_tensor(gaps[0][:], v_psum[0], picked0[:], ALU.subtract)
+        scatter(0, gates[:, 0, :])
+
+        nc.scalar.copy(out=values23[:], in_=v_banks[2][:])
+        nc.scalar.copy(out=value1[:], in_=v_psum[1])
+        nc.scalar.activation(neg_gates[:], gates[:, 1:, :], ACT.Copy, scale=-1.0)
+
+        add_on_tensor(0, ("bank2", "bank3"), ("bank5", "bank6"))
+        for r in gather_order:
+            nc.vector.tensor_tensor(gaps[r][:], pages[r][:].indirect(offsets[:]), values[r], ALU.subtract)
+        clear_late(2)
+        scatter(1, neg_gates[:, 0, :])
+        clear_late(3)
+        add_on_tensor(1, ("bank5", "bank6"), ("bank2", "bank3"))
+        scatter(2, neg_gates[:, 1, :])
+        add_on_vector(2, 0, T)
+        scatter(3, neg_gates[:, 2, :])
+        add_on_vector(3, 0, LAST_CUT)
+        add_on_vector(3, LAST_CUT, T)

from contextlib import ExitStack

import concourse.mybir as mybir
from concourse.masks import make_identity

K, T, J, N, L = 512, 1024, 256, 512, 512
FLOPS = 2 * K * N * J + 2 * L * N * J

F32 = mybir.dt.float32
BF16 = mybir.dt.bfloat16
I32 = mybir.dt.int32
U32 = mybir.dt.uint32
U16 = mybir.dt.uint16
U8 = mybir.dt.uint8
FP8X4 = mybir.dt.float8_e4m3fn_x4
FP4X4 = mybir.dt.float4_e2m1fn_x4
ALU = mybir.AluOpType
ACT = mybir.ActivationFunctionType

P = 128
PACK = 4
SLICES = N // P
BANK = 512
LINE = 4
VECTOR_SHARE = 68
LAST_CUT = 640


def load_plane(nc, plane, scales):
    rows = scales[0].bitcast(I32)
    words = plane[:].bitcast(I32)
    for q in range(4):
        nc.sync.dma_start(words[32 * q : 32 * q + 4, :], rows[4 * q : 4 * q + 4, :])


def tile_list_head_page_drift_kernel(tc, xv_words, xv_scales, wv, xg_words, xg_scales, wg_words, wg_scales, old, offs, out):
    nc = tc.nc
    with ExitStack() as ctx:
        keep = ctx.enter_context(tc.tile_pool(name="keep", bufs=1))
        psum = ctx.enter_context(tc.psum_pool(name="psum", bufs=1))

        offsets = keep.tile([P, J // 16], U16, name="offsets")
        wv_raw = keep.tile([P, PACK, N], F32, name="wv_raw")
        wv_bf = keep.tile([P, SLICES, P, PACK], BF16, name="wv_bf", align_bytes=64)
        wv_codes = keep.tile([P, N], U32, name="wv_codes", align_bytes=64)
        wv_plane = keep.tile([P, N], U8, name="wv_plane", align_bytes=64)
        wg_codes_raw = keep.tile([P, N], I32, name="wg_codes_raw")
        wg_plane_raw = keep.tile([P, N], U8, name="wg_plane_raw")
        wg_codes = keep.tile([P, N], I32, name="wg_codes", align_bytes=64)
        wg_plane = keep.tile([P, N], U8, name="wg_plane", align_bytes=64)
        xv_codes = keep.tile([P, J], I32, name="xv_codes", align_bytes=64)
        xv_plane = keep.tile([P, J], U8, name="xv_plane", align_bytes=64)
        xg_codes = keep.tile([P, 2 * J], U8, name="xg_codes", align_bytes=64)
        xg_plane = keep.tile([P, J], U8, name="xg_plane", align_bytes=64)
        pages = [keep.tile([P, T], F32, name=f"page{r}") for r in range(SLICES)]
        results = [keep.tile([P, T], F32, name=f"result{r}") for r in range(SLICES)]
        gates = keep.tile([P, SLICES, J], F32, name="gates")
        picked0 = keep.tile([P, J], F32, name="picked0")
        neg_gates = keep.tile([P, SLICES - 1, J], F32, name="neg_gates")
        value1 = keep.tile([P, J], F32, name="value1", tag="then_drift2")
        values23 = keep.tile([P, 2, J], F32, name="values23")
        values = {1: value1[:], 2: values23[:, 0, :], 3: values23[:, 1, :]}
        gaps = [keep.tile([P, J], F32, name=f"gap{r}", tag="then_drift3" if r == 1 else f"gap{r}") for r in range(SLICES)]
        g_banks = [psum.tile([P, 2, J], F32, name=f"g_bank{h}", tag=f"bank{h}") for h in range(2)]
        v_banks = [psum.tile([P, 2, J], F32, name=f"v_bank{h}", tag=f"bank{2 + h}") for h in range(3)]
        v_psum = [v_banks[0][:, 0, :], v_banks[1][:, 0, :], v_banks[2][:, 0, :], v_banks[2][:, 1, :]]

        old_slices = old.rearrange("(p r) t -> r p t", r=SLICES)
        out_slices = out.rearrange("(p r) t -> r p t", r=SLICES)

        for plane in (wg_plane_raw, xv_plane, xg_plane):
            nc.vector.memset(plane[:].bitcast(U32), 0)

        nc.sync.dma_start(wg_codes_raw[:], wg_words[0].rearrange("p n t -> p (n t)").bitcast(I32))
        nc.sync.dma_start(offsets[:], offs)
        nc.sync.dma_start(xg_codes[:].bitcast(I32), xg_words[0].bitcast(I32))
        load_plane(nc, wg_plane_raw, wg_scales)
        nc.sync.dma_start(wv_raw[:], wv.rearrange("(p j) n -> p j n", j=PACK))
        load_plane(nc, xg_plane, xg_scales)
        nc.sync.dma_start(xv_codes[:], xv_words[0].rearrange("p n t -> p (n t)").bitcast(I32))
        nc.sync.dma_start(pages[0][:], old_slices[0])
        load_plane(nc, xv_plane, xv_scales)
        gather_order = (2, 3, 1)
        for r in gather_order:
            nc.sync.dma_start(pages[r][:], old_slices[r])

        identity = keep.tile([P, P], F32, name="identity")
        make_identity(nc, identity[:])
        drifts = [keep.tile([P, T], F32, name=f"drift{r}") for r in range(2)]
        for r in range(2):
            nc.vector.memset(drifts[r][:], 0.0)

        src = wv_raw[:].rearrange("p j (m r) -> p m r j", r=SLICES)
        dst = wv_bf[:].rearrange("p r m j -> p m r j")
        nc.vector.tensor_copy(out=dst[:, :VECTOR_SHARE], in_=src[:, :VECTOR_SHARE])
        nc.scalar.copy(out=dst[:, VECTOR_SHARE:], in_=src[:, VECTOR_SHARE:])

        nc.vector.tensor_copy(
            out=wg_codes[:].rearrange("p (r c i) -> p c r i", r=SLICES, i=LINE),
            in_=wg_codes_raw[:].rearrange("p (c i r) -> p c r i", r=SLICES, i=LINE),
        )
        nc.vector.tensor_copy(
            out=wg_plane[:].rearrange("p (r m) -> p r m", r=SLICES),
            in_=wg_plane_raw[:].rearrange("p (m r) -> p r m", r=SLICES),
        )

        for lo, hi in ((0, 1), (1, 2), (2, 4)):
            nc.vector.quantize_mx(
                out=wv_codes[:, lo * P : hi * P].bitcast(FP8X4),
                scales=wv_plane[:, lo * P : hi * P],
                in_=wv_bf[:, lo:hi].rearrange("p r m j -> p (r m j)"),
            )

        def product(acc, r, w_codes, w_plane, x_codes, x_plane):
            cols = slice(r * P, (r + 1) * P)
            nc.tensor.matmul_mx(
                out=acc,
                lhsT=w_codes[:, cols].bitcast(FP8X4),
                lhsT_scale=w_plane[:, cols],
                rhs=x_codes,
                rhs_scale=x_plane[:],
                start=True,
                stop=True,
            )

        for h in range(2):
            for e in range(2):
                product(g_banks[h][:, e, :], 2 * h + e, wg_codes, wg_plane, xg_codes[:].bitcast(FP4X4), xg_plane)
            nc.scalar.activation(gates[:, 2 * h : 2 * h + 2, :], g_banks[h][:], ACT.Sigmoid)
        for r in range(SLICES):
            product(v_psum[r], r, wv_codes, wv_plane, xv_codes[:].bitcast(FP8X4), xv_plane)

        def scatter(r, factor):
            nc.vector.tensor_tensor(drifts[r][:].indirect(offsets[:]), gaps[r][:], factor, ALU.mult)

        def clear_late(r):
            drifts.append(keep.tile([P, T], F32, name=f"drift{r}", tag=f"then_drift{r}"))
            nc.gpsimd.memset(drifts[r][:], 0.0)

        def add_on_vector(r, lo, hi):
            nc.vector.tensor_tensor(results[r][:, lo:hi], pages[r][:, lo:hi], drifts[r][:, lo:hi], ALU.add)
            nc.sync.dma_start(out_slices[r][:, lo:hi], results[r][:, lo:hi])

        def add_on_tensor(r, sum_tags, back_tags):
            blocks = BANK // P
            halves = range(T // BANK)
            sums = [psum.tile([P, blocks, P], F32, name=f"sums{r}{h}", tag=sum_tags[h]) for h in halves]
            for k, term in enumerate((pages[r], drifts[r])):
                for h in halves:
                    for b in range(blocks):
                        first = h * BANK + b * P
                        nc.tensor.matmul(
                            sums[h][:, b, :],
                            term[:, first : first + P],
                            identity[:],
                            is_transpose=True,
                            start=(k == 0 and b == 0),
                            stop=(k == 1 and b == blocks - 1),
                        )
            turned = [keep.tile([P, blocks, P], F32, name=f"turned{r}{h}") for h in halves]
            for h in halves:
                nc.scalar.copy(out=turned[h][:], in_=sums[h][:])
            for h in halves:
                back = psum.tile([P, blocks, P], F32, name=f"back{r}{h}", tag=back_tags[h])
                for b in range(blocks):
                    nc.tensor.transpose(back[:, b, :], turned[h][:, b, :], identity[:])
                cols = slice(h * BANK, (h + 1) * BANK)
                nc.scalar.copy(out=results[r][:, cols], in_=back[:].rearrange("p b c -> p (b c)"))
                nc.scalar.dma_start(out_slices[r][:, cols], results[r][:, cols])

        nc.vector.tensor_copy(picked0[:], pages[0][:].indirect(offsets[:]))
        nc.vector.tensor_tensor(gaps[0][:], v_psum[0], picked0[:], ALU.subtract)
        scatter(0, gates[:, 0, :])

        nc.scalar.copy(out=values23[:], in_=v_banks[2][:])
        nc.scalar.copy(out=value1[:], in_=v_psum[1])
        nc.scalar.activation(neg_gates[:], gates[:, 1:, :], ACT.Copy, scale=-1.0)

        add_on_tensor(0, ("bank2", "bank3"), ("bank5", "bank6"))
        for r in gather_order:
            nc.vector.tensor_tensor(gaps[r][:], pages[r][:].indirect(offsets[:]), values[r], ALU.subtract)
        clear_late(2)
        scatter(1, neg_gates[:, 0, :])
        clear_late(3)
        add_on_tensor(1, ("bank5", "bank6"), ("bank2", "bank3"))
        scatter(2, neg_gates[:, 1, :])
        add_on_vector(2, 0, T)
        scatter(3, neg_gates[:, 2, :])
        add_on_vector(3, 0, LAST_CUT)
        add_on_vector(3, LAST_CUT, T)
